import numpy as np
CORES = [10,114,138,242]
N = 4
def setup_inputs(rng):
    return {"x": rng.standard_normal((N, 32, 1024), dtype=np.float32)}
def reference(x):
    s = x.sum(axis=0, dtype=np.float64).astype(x.dtype)
    return {"y": np.broadcast_to(s, (N,) + s.shape)}

@@ -1,0 +1,67 @@
+from concourse.bass import DstId, RemoteDMATransfer
+R = 4
+NP = 16
+W = 256 // NP
+SCRATCH = {'s': ('dram', [NP, 128, W], 'float32'), 'p': ('dram', [2 * R, 128, W], 'float32'), 'r': ('dram', [NP, 128, W], 'float32')}
+SEMAPHORES = ['loaded', 'sent', 'arrived', 'result', 'stored']
+A_CORE = 4
+B_CORES = [1, 5]
+OFF = [[[3, 12], [16, 32], [64, 128]], [[1, 2], [4, 8], [48, 192]]]
+ON = [3840, 61440]
+
+def bits(m):
+    return bin(m).count('1')
+
+def place(k):
+    return (k // 8, k % 8 // 2, k % 2)
+
+def reducer(cores, k):
+    wave, q, j = place(k)
+    if wave == 0:
+        return (cores[q] + A_CORE, j)
+    return (cores[q] + B_CORES[j], 0)
+
+def send_mask(i, k):
+    wave, q, j = place(k)
+    if q == i:
+        return ON[j]
+    others = [(i + 1 + t) % R for t in range(R - 1)]
+    return OFF[wave][others.index(q)][j]
+
+def rank_program(g, core, T, topo):
+    cores = list(T.cores)
+    rank = T.rank_of(core)
+
+    def dst_id(d):
+        rid, pid = topo.addr(d, core)
+        return DstId(rid=rid, pnc=pid)
+    if rank is not None:
+        g.dma_start(T.s[:], T.x[:]).then_inc(T.sem.loaded, 16)
+        g.wait_ge(T.sem.loaded, 16)
+        for wave in range(2):
+            trs = []
+            for k in range(8 * wave, 8 * wave + 8):
+                h, slot = reducer(cores, k)
+                trs.append(RemoteDMATransfer(dst_ids=[dst_id(h)], dma_engine_mask=send_mask(rank, k), remote_sem=T.sem.arrived, src=T.s[k], dst=T.p[slot * R + rank]))
+            g.remote_dma_fused(trs, local_sem=T.sem.sent)
+        g.wait_ge(T.sem.result, 8 * 4 + 8 * 8)
+        g.dma_start(T.y[:], T.r[:]).then_inc(T.sem.stored, 16)
+        g.wait_ge(T.sem.sent, sum((bits(send_mask(rank, k)) for k in range(NP))))
+        g.wait_ge(T.sem.stored, 16)
+        return
+    mine = [k for k in range(NP) if reducer(cores, k)[0] == core]
+    if not mine:
+        return
+    home = cores[place(mine[0])[1]]
+    away = [c for c in cores if c != home]
+    g.wait_ge(T.sem.arrived, sum((bits(send_mask(i, k)) for k in mine for i in range(R))))
+    n = 8 // len(mine)
+    trs = []
+    for t, k in enumerate(mine):
+        slot = reducer(cores, k)[1]
+        srcs = [T.p[slot * R + i] for i in range(R)]
+        m = (1 << n) - 1 << n * t
+        trs.append(RemoteDMATransfer(dst_ids=[dst_id(c) for c in away], dma_engine_mask=m, remote_sem=T.sem.result, srcs=srcs, dsts=[T.r[k] for c in away], alu_op=1))
+        trs.append(RemoteDMATransfer(dst_ids=[dst_id(home)], dma_engine_mask=m << 8, remote_sem=T.sem.result, srcs=srcs, dsts=[T.r[k]], alu_op=1))
+    g.remote_dma_fused(trs, local_sem=T.sem.sent)
+    g.wait_ge(T.sem.sent, 16)

@@ -3,7 +3,7 @@ R = 4
 NP = 16
 W = 256 // NP
 SCRATCH = {'s': ('dram', [NP, 128, W], 'float32'), 'p': ('dram', [2 * R, 128, W], 'float32'), 'r': ('dram', [NP, 128, W], 'float32')}
-SEMAPHORES = ['loaded', 'sent', 'arrived', 'result', 'stored']
+SEMAPHORES = ['ld0', 'ld1', 'sent', 'arrived', 'res0', 'res1', 'stored']
 A_CORE = 4
 B_CORES = [1, 5]
 OFF = [[[3, 12], [16, 32], [64, 128]], [[1, 2], [4, 8], [48, 192]]]
@@ -36,22 +36,29 @@ def rank_program(g, core, T, topo):
         rid, pid = topo.addr(d, core)
         return DstId(rid=rid, pnc=pid)
     if rank is not None:
-        g.dma_start(T.s[:], T.x[:]).then_inc(T.sem.loaded, 16)
-        g.wait_ge(T.sem.loaded, 16)
+        lds = [T.sem.ld0, T.sem.ld1]
+        res = [T.sem.res0, T.sem.res1]
+        qs = [g.sync, g.scalar]
         for wave in range(2):
+            qs[wave].dma_start(T.s[8 * wave:8 * wave + 8], T.x[16 * wave:16 * wave + 16]).then_inc(lds[wave], 16)
+        for wave in range(2):
+            g.wait_ge(lds[wave], 16)
             trs = []
             for k in range(8 * wave, 8 * wave + 8):
                 h, slot = reducer(cores, k)
                 trs.append(RemoteDMATransfer(dst_ids=[dst_id(h)], dma_engine_mask=send_mask(rank, k), remote_sem=T.sem.arrived, src=T.s[k], dst=T.p[slot * R + rank]))
             g.remote_dma_fused(trs, local_sem=T.sem.sent)
-        g.wait_ge(T.sem.result, 8 * 4 + 8 * 8)
-        g.dma_start(T.y[:], T.r[:]).then_inc(T.sem.stored, 16)
+        for wave in range(2):
+            qs[wave].wait_ge(res[wave], 8 * 4 * (wave + 1))
+            qs[wave].dma_start(T.y[16 * wave:16 * wave + 16], T.r[8 * wave:8 * wave + 8]).then_inc(T.sem.stored, 16)
         g.wait_ge(T.sem.sent, sum((bits(send_mask(rank, k)) for k in range(NP))))
-        g.wait_ge(T.sem.stored, 16)
+        g.wait_ge(T.sem.stored, 32)
         return
     mine = [k for k in range(NP) if reducer(cores, k)[0] == core]
     if not mine:
         return
+    wave = place(mine[0])[0]
+    rsem = [T.sem.res0, T.sem.res1][wave]
     home = cores[place(mine[0])[1]]
     away = [c for c in cores if c != home]
     g.wait_ge(T.sem.arrived, sum((bits(send_mask(i, k)) for k in mine for i in range(R))))
@@ -61,7 +68,7 @@ def rank_program(g, core, T, topo):
         slot = reducer(cores, k)[1]
         srcs = [T.p[slot * R + i] for i in range(R)]
         m = (1 << n) - 1 << n * t
-        trs.append(RemoteDMATransfer(dst_ids=[dst_id(c) for c in away], dma_engine_mask=m, remote_sem=T.sem.result, srcs=srcs, dsts=[T.r[k] for c in away], alu_op=1))
-        trs.append(RemoteDMATransfer(dst_ids=[dst_id(home)], dma_engine_mask=m << 8, remote_sem=T.sem.result, srcs=srcs, dsts=[T.r[k]], alu_op=1))
+        trs.append(RemoteDMATransfer(dst_ids=[dst_id(c) for c in away], dma_engine_mask=m, remote_sem=rsem, srcs=srcs, dsts=[T.r[k] for c in away], alu_op=1))
+        trs.append(RemoteDMATransfer(dst_ids=[dst_id(home)], dma_engine_mask=m << 8, remote_sem=rsem, srcs=srcs, dsts=[T.r[k]], alu_op=1))
     g.remote_dma_fused(trs, local_sem=T.sem.sent)
     g.wait_ge(T.sem.sent, 16)

@@ -2,31 +2,19 @@ from concourse.bass import DstId, RemoteDMATransfer
 R = 4
 NP = 16
 W = 256 // NP
-SCRATCH = {'s': ('dram', [NP, 128, W], 'float32'), 'p': ('dram', [2 * R, 128, W], 'float32'), 'r': ('dram', [NP, 128, W], 'float32')}
+SCRATCH = {'s': ('dram', [NP, 128, W], 'float32'), 'p': ('dram', [R, 128, W], 'float32'), 'r': ('dram', [NP, 128, W], 'float32')}
 SEMAPHORES = ['ld0', 'ld1', 'sent', 'arrived', 'res0', 'res1', 'stored']
-A_CORE = 4
-B_CORES = [1, 5]
-OFF = [[[3, 12], [16, 32], [64, 128]], [[1, 2], [4, 8], [48, 192]]]
-ON = [3840, 61440]
 
-def bits(m):
-    return bin(m).count('1')
 
-def place(k):
-    return (k // 8, k % 8 // 2, k % 2)
+def reducer(k):
+    wave, t = k // 8, k % 8
+    parity, die, host = t % 2, (t // 2) % 2, t // 4
+    chip = 2 + parity + 2 * (wave * 2 + die)
+    return host * 128 + chip * 8 + (6 if die == 0 else 3)
 
-def reducer(cores, k):
-    wave, q, j = place(k)
-    if wave == 0:
-        return (cores[q] + A_CORE, j)
-    return (cores[q] + B_CORES[j], 0)
 
-def send_mask(i, k):
-    wave, q, j = place(k)
-    if q == i:
-        return ON[j]
-    others = [(i + 1 + t) % R for t in range(R - 1)]
-    return OFF[wave][others.index(q)][j]
+RED = [reducer(k) for k in range(NP)]
+
 
 def rank_program(g, core, T, topo):
     cores = list(T.cores)
@@ -35,40 +23,30 @@ def rank_program(g, core, T, topo):
     def dst_id(d):
         rid, pid = topo.addr(d, core)
         return DstId(rid=rid, pnc=pid)
+    res = [T.sem.res0, T.sem.res1]
     if rank is not None:
         lds = [T.sem.ld0, T.sem.ld1]
-        res = [T.sem.res0, T.sem.res1]
         qs = [g.sync, g.scalar]
         for wave in range(2):
             qs[wave].dma_start(T.s[8 * wave:8 * wave + 8], T.x[16 * wave:16 * wave + 16]).then_inc(lds[wave], 16)
         for wave in range(2):
             g.wait_ge(lds[wave], 16)
             trs = []
-            for k in range(8 * wave, 8 * wave + 8):
-                h, slot = reducer(cores, k)
-                trs.append(RemoteDMATransfer(dst_ids=[dst_id(h)], dma_engine_mask=send_mask(rank, k), remote_sem=T.sem.arrived, src=T.s[k], dst=T.p[slot * R + rank]))
+            for t in range(8):
+                k = 8 * wave + t
+                trs.append(RemoteDMATransfer(dst_ids=[dst_id(RED[k])], dma_engine_mask=1 << t, remote_sem=T.sem.arrived, src=T.s[k], dst=T.p[rank]))
             g.remote_dma_fused(trs, local_sem=T.sem.sent)
         for wave in range(2):
-            qs[wave].wait_ge(res[wave], 8 * 4 * (wave + 1))
+            qs[wave].wait_ge(res[wave], 64)
             qs[wave].dma_start(T.y[16 * wave:16 * wave + 16], T.r[8 * wave:8 * wave + 8]).then_inc(T.sem.stored, 16)
-        g.wait_ge(T.sem.sent, sum((bits(send_mask(rank, k)) for k in range(NP))))
+        g.wait_ge(T.sem.sent, 16)
         g.wait_ge(T.sem.stored, 32)
         return
-    mine = [k for k in range(NP) if reducer(cores, k)[0] == core]
-    if not mine:
+    if core not in RED:
         return
-    wave = place(mine[0])[0]
-    rsem = [T.sem.res0, T.sem.res1][wave]
-    home = cores[place(mine[0])[1]]
-    away = [c for c in cores if c != home]
-    g.wait_ge(T.sem.arrived, sum((bits(send_mask(i, k)) for k in mine for i in range(R))))
-    n = 8 // len(mine)
-    trs = []
-    for t, k in enumerate(mine):
-        slot = reducer(cores, k)[1]
-        srcs = [T.p[slot * R + i] for i in range(R)]
-        m = (1 << n) - 1 << n * t
-        trs.append(RemoteDMATransfer(dst_ids=[dst_id(c) for c in away], dma_engine_mask=m, remote_sem=rsem, srcs=srcs, dsts=[T.r[k] for c in away], alu_op=1))
-        trs.append(RemoteDMATransfer(dst_ids=[dst_id(home)], dma_engine_mask=m << 8, remote_sem=rsem, srcs=srcs, dsts=[T.r[k]], alu_op=1))
+    k = RED.index(core)
+    g.wait_ge(T.sem.arrived, R)
+    srcs = [T.p[i] for i in range(R)]
+    trs = [RemoteDMATransfer(dst_ids=[dst_id(c) for c in cores], dma_engine_mask=0xFF, remote_sem=res[k // 8], srcs=srcs, dsts=[T.r[k] for c in cores], alu_op=1)]
     g.remote_dma_fused(trs, local_sem=T.sem.sent)
-    g.wait_ge(T.sem.sent, 16)
+    g.wait_ge(T.sem.sent, 8)

@@ -1,19 +1,36 @@
 from concourse.bass import DstId, RemoteDMATransfer
 R = 4
-NP = 16
-W = 256 // NP
-SCRATCH = {'s': ('dram', [NP, 128, W], 'float32'), 'p': ('dram', [R, 128, W], 'float32'), 'r': ('dram', [NP, 128, W], 'float32')}
-SEMAPHORES = ['ld0', 'ld1', 'sent', 'arrived', 'res0', 'res1', 'stored']
+NW = 2
+PW = 8
+WS = [20, 12]
+CORES = [10, 114, 138, 242]
+SCRATCH = {'s0': ('dram', [PW, 128, WS[0]], 'float32'), 's1': ('dram', [PW, 128, WS[1]], 'float32'),
+           'p0': ('dram', [R, 128, WS[0]], 'float32'), 'p1': ('dram', [R, 128, WS[1]], 'float32'),
+           'r0': ('dram', [PW, 128, WS[0]], 'float32'), 'r1': ('dram', [PW, 128, WS[1]], 'float32')}
+SEMAPHORES = ['sent', 'arrived', 'stored', 'ld0', 'ld1', 'res0', 'res1']
+DIE_CORE = [6, 3]
 
 
-def reducer(k):
-    wave, t = k // 8, k % 8
-    parity, die, host = t % 2, (t // 2) % 2, t // 4
-    chip = 2 + parity + 2 * (wave * 2 + die)
-    return host * 128 + chip * 8 + (6 if die == 0 else 3)
+def reducer(w, t):
+    base = CORES[t % R] - CORES[t % R] % 8
+    if t < R:
+        return base + DIE_CORE[w]
+    return (base ^ 8) + DIE_CORE[1 - w]
 
 
-RED = [reducer(k) for k in range(NP)]
+RED = [reducer(w, t) for w in range(NW) for t in range(PW)]
+
+
+def bits(m):
+    return bin(m).count('1')
+
+
+def send_mask(i, t):
+    if t == i:
+        return 0xFF00
+    off = [u for u in range(PW) if u != i]
+    j = off.index(t)
+    return 0xC0 if j == 6 else 1 << j
 
 
 def rank_program(g, core, T, topo):
@@ -24,29 +41,34 @@ def rank_program(g, core, T, topo):
         rid, pid = topo.addr(d, core)
         return DstId(rid=rid, pnc=pid)
     res = [T.sem.res0, T.sem.res1]
+    ss, ps, rs = [T.s0, T.s1], [T.p0, T.p1], [T.r0, T.r1]
     if rank is not None:
         lds = [T.sem.ld0, T.sem.ld1]
         qs = [g.sync, g.scalar]
-        for wave in range(2):
-            qs[wave].dma_start(T.s[8 * wave:8 * wave + 8], T.x[16 * wave:16 * wave + 16]).then_inc(lds[wave], 16)
-        for wave in range(2):
-            g.wait_ge(lds[wave], 16)
+        rows = [(0, WS[0]), (WS[0], 32)]
+        for w in range(NW):
+            qs[w].dma_start(ss[w][:], T.x[rows[w][0]:rows[w][1]]).then_inc(lds[w], 16)
+        for w in range(NW):
+            g.wait_ge(lds[w], 16)
             trs = []
-            for t in range(8):
-                k = 8 * wave + t
-                trs.append(RemoteDMATransfer(dst_ids=[dst_id(RED[k])], dma_engine_mask=1 << t, remote_sem=T.sem.arrived, src=T.s[k], dst=T.p[rank]))
+            for t in range(PW):
+                trs.append(RemoteDMATransfer(dst_ids=[dst_id(RED[PW * w + t])], dma_engine_mask=send_mask(rank, t), remote_sem=T.sem.arrived, src=ss[w][t], dst=ps[w][rank]))
             g.remote_dma_fused(trs, local_sem=T.sem.sent)
-        for wave in range(2):
-            qs[wave].wait_ge(res[wave], 64)
-            qs[wave].dma_start(T.y[16 * wave:16 * wave + 16], T.r[8 * wave:8 * wave + 8]).then_inc(T.sem.stored, 16)
-        g.wait_ge(T.sem.sent, 16)
-        g.wait_ge(T.sem.stored, 32)
+        for w in range(NW):
+            qs[w].wait_ge(res[w], 8 * PW)
+            qs[w].dma_start(T.y[rows[w][0]:rows[w][1]], rs[w][:]).then_inc(T.sem.stored, 16)
+        g.wait_ge(T.sem.sent, NW * sum(bits(send_mask(rank, t)) for t in range(PW)))
+        g.wait_ge(T.sem.stored, 16 * NW)
         return
     if core not in RED:
         return
-    k = RED.index(core)
-    g.wait_ge(T.sem.arrived, R)
-    srcs = [T.p[i] for i in range(R)]
-    trs = [RemoteDMATransfer(dst_ids=[dst_id(c) for c in cores], dma_engine_mask=0xFF, remote_sem=res[k // 8], srcs=srcs, dsts=[T.r[k] for c in cores], alu_op=1)]
+    w, t = RED.index(core) // PW, RED.index(core) % PW
+    g.wait_ge(T.sem.arrived, sum(bits(send_mask(i, t)) for i in range(R)))
+    srcs = [ps[w][i] for i in range(R)]
+    away = [c for c in cores if c // 8 != core // 8]
+    home = [c for c in cores if c // 8 == core // 8]
+    trs = [RemoteDMATransfer(dst_ids=[dst_id(c) for c in away], dma_engine_mask=0xFF, remote_sem=res[w], srcs=srcs, dsts=[rs[w][t] for c in away], alu_op=1)]
+    if home:
+        trs.append(RemoteDMATransfer(dst_ids=[dst_id(c) for c in home], dma_engine_mask=0xFF00, remote_sem=res[w], srcs=srcs, dsts=[rs[w][t] for c in home], alu_op=1))
     g.remote_dma_fused(trs, local_sem=T.sem.sent)
-    g.wait_ge(T.sem.sent, 8)
+    g.wait_ge(T.sem.sent, 8 * len(trs))

@@ -1,35 +1,33 @@
 from concourse.bass import DstId, RemoteDMATransfer
 R = 4
 NW = 2
-PW = 8
-WS = [20, 12]
+PWS = [10, 8]
+WS = [16, 12]
+ROWS = [PWS[w] * WS[w] // 8 for w in range(NW)]
+assert sum(ROWS) == 32
 CORES = [10, 114, 138, 242]
-SCRATCH = {'s0': ('dram', [PW, 128, WS[0]], 'float32'), 's1': ('dram', [PW, 128, WS[1]], 'float32'),
+SCRATCH = {'s0': ('dram', [PWS[0], 128, WS[0]], 'float32'), 's1': ('dram', [PWS[1], 128, WS[1]], 'float32'),
            'p0': ('dram', [R, 128, WS[0]], 'float32'), 'p1': ('dram', [R, 128, WS[1]], 'float32'),
-           'r0': ('dram', [PW, 128, WS[0]], 'float32'), 'r1': ('dram', [PW, 128, WS[1]], 'float32')}
+           'r0': ('dram', [PWS[0], 128, WS[0]], 'float32'), 'r1': ('dram', [PWS[1], 128, WS[1]], 'float32')}
 SEMAPHORES = ['sent', 'arrived', 'stored', 'ld0', 'ld1', 'res0', 'res1']
-DIE_CORE = [6, 3]
-
-
-def reducer(w, t):
-    base = CORES[t % R] - CORES[t % R] % 8
-    if t < R:
-        return base + DIE_CORE[w]
-    return (base ^ 8) + DIE_CORE[1 - w]
-
-
-RED = [reducer(w, t) for w in range(NW) for t in range(PW)]
+BASE = [c - c % 8 for c in CORES]
+RED = [[BASE[q] + 6 for q in range(R)] + [BASE[q] + 3 for q in range(R)] + [(BASE[0] ^ 8) + 6, (BASE[1] ^ 8) + 2],
+       [BASE[q] + 7 for q in range(R)] + [(BASE[q] ^ 8) + 3 for q in range(R)]]
 
 
 def bits(m):
     return bin(m).count('1')
 
 
-def send_mask(i, t):
-    if t == i:
-        return 0xFF00
-    off = [u for u in range(PW) if u != i]
+def send_mask(i, w, t):
+    on = [u for u in range(PWS[w]) if RED[w][u] // 8 == CORES[i] // 8]
+    off = [u for u in range(PWS[w]) if RED[w][u] // 8 != CORES[i] // 8]
+    if t in on:
+        n = 8 // len(on)
+        return ((1 << n) - 1) << (8 + n * on.index(t))
     j = off.index(t)
+    if len(off) == 8:
+        return 1 << j
     return 0xC0 if j == 6 else 1 << j
 
 
@@ -45,25 +43,26 @@ def rank_program(g, core, T, topo):
     if rank is not None:
         lds = [T.sem.ld0, T.sem.ld1]
         qs = [g.sync, g.scalar]
-        rows = [(0, WS[0]), (WS[0], 32)]
+        rows = [(0, ROWS[0]), (ROWS[0], 32)]
         for w in range(NW):
             qs[w].dma_start(ss[w][:], T.x[rows[w][0]:rows[w][1]]).then_inc(lds[w], 16)
         for w in range(NW):
             g.wait_ge(lds[w], 16)
             trs = []
-            for t in range(PW):
-                trs.append(RemoteDMATransfer(dst_ids=[dst_id(RED[PW * w + t])], dma_engine_mask=send_mask(rank, t), remote_sem=T.sem.arrived, src=ss[w][t], dst=ps[w][rank]))
+            for t in range(PWS[w]):
+                trs.append(RemoteDMATransfer(dst_ids=[dst_id(RED[w][t])], dma_engine_mask=send_mask(rank, w, t), remote_sem=T.sem.arrived, src=ss[w][t], dst=ps[w][rank]))
             g.remote_dma_fused(trs, local_sem=T.sem.sent)
         for w in range(NW):
-            qs[w].wait_ge(res[w], 8 * PW)
+            qs[w].wait_ge(res[w], 8 * PWS[w])
             qs[w].dma_start(T.y[rows[w][0]:rows[w][1]], rs[w][:]).then_inc(T.sem.stored, 16)
-        g.wait_ge(T.sem.sent, NW * sum(bits(send_mask(rank, t)) for t in range(PW)))
+        g.wait_ge(T.sem.sent, sum(bits(send_mask(rank, w, t)) for w in range(NW) for t in range(PWS[w])))
         g.wait_ge(T.sem.stored, 16 * NW)
         return
-    if core not in RED:
+    mine = [(w, t) for w in range(NW) for t in range(PWS[w]) if RED[w][t] == core]
+    if not mine:
         return
-    w, t = RED.index(core) // PW, RED.index(core) % PW
-    g.wait_ge(T.sem.arrived, sum(bits(send_mask(i, t)) for i in range(R)))
+    w, t = mine[0]
+    g.wait_ge(T.sem.arrived, sum(bits(send_mask(i, w, t)) for i in range(R)))
     srcs = [ps[w][i] for i in range(R)]
     away = [c for c in cores if c // 8 != core // 8]
     home = [c for c in cores if c // 8 == core // 8]

@@ -19,16 +19,27 @@ def bits(m):
     return bin(m).count('1')
 
 
+def hops(i, c):
+    a, b = CORES[i] // 8, c // 8
+    if a == b:
+        return 0
+    return 2 if (a % 2 != b % 2 and a ^ 1 != b) else 1
+
+
+def order(i, w):
+    return sorted(range(PWS[w]), key=lambda u: (-hops(i, RED[w][u]), u))
+
+
 def send_mask(i, w, t):
-    on = [u for u in range(PWS[w]) if RED[w][u] // 8 == CORES[i] // 8]
-    off = [u for u in range(PWS[w]) if RED[w][u] // 8 != CORES[i] // 8]
+    on = [u for u in order(i, w) if hops(i, RED[w][u]) == 0]
+    off = [u for u in order(i, w) if hops(i, RED[w][u]) > 0]
     if t in on:
         n = 8 // len(on)
         return ((1 << n) - 1) << (8 + n * on.index(t))
     j = off.index(t)
     if len(off) == 8:
         return 1 << j
-    return 0xC0 if j == 6 else 1 << j
+    return 3 if j == 0 else 1 << (j + 1)
 
 
 def rank_program(g, core, T, topo):
@@ -45,11 +56,11 @@ def rank_program(g, core, T, topo):
         qs = [g.sync, g.scalar]
         rows = [(0, ROWS[0]), (ROWS[0], 32)]
         for w in range(NW):
-            qs[w].dma_start(ss[w][:], T.x[rows[w][0]:rows[w][1]]).then_inc(lds[w], 16)
+            g.sync.dma_start(ss[w][:], T.x[rows[w][0]:rows[w][1]]).then_inc(lds[w], 16)
         for w in range(NW):
             g.wait_ge(lds[w], 16)
             trs = []
-            for t in range(PWS[w]):
+            for t in order(rank, w):
                 trs.append(RemoteDMATransfer(dst_ids=[dst_id(RED[w][t])], dma_engine_mask=send_mask(rank, w, t), remote_sem=T.sem.arrived, src=ss[w][t], dst=ps[w][rank]))
             g.remote_dma_fused(trs, local_sem=T.sem.sent)
         for w in range(NW):

from concourse.bass import DstId, RemoteDMATransfer
R = 4
NW = 2
PWS = [10, 8]
WS = [16, 12]
ROWS = [PWS[w] * WS[w] // 8 for w in range(NW)]
assert sum(ROWS) == 32
CORES = [10, 114, 138, 242]
SCRATCH = {'s0': ('dram', [PWS[0], 128, WS[0]], 'float32'), 's1': ('dram', [PWS[1], 128, WS[1]], 'float32'),
           'p0': ('dram', [R, 128, WS[0]], 'float32'), 'p1': ('dram', [R, 128, WS[1]], 'float32'),
           'r0': ('dram', [PWS[0], 128, WS[0]], 'float32'), 'r1': ('dram', [PWS[1], 128, WS[1]], 'float32')}
SEMAPHORES = ['sent', 'arrived', 'stored', 'ld0', 'ld1', 'res0', 'res1']
BASE = [c - c % 8 for c in CORES]
RED = [[BASE[q] + 6 for q in range(R)] + [BASE[q] + 3 for q in range(R)] + [(BASE[0] ^ 8) + 6, (BASE[1] ^ 8) + 2],
       [BASE[q] + 7 for q in range(R)] + [(BASE[q] ^ 8) + 3 for q in range(R)]]


def bits(m):
    return bin(m).count('1')


def hops(i, c):
    a, b = CORES[i] // 8, c // 8
    if a == b:
        return 0
    return 2 if (a % 2 != b % 2 and a ^ 1 != b) else 1


def order(i, w):
    return sorted(range(PWS[w]), key=lambda u: (-hops(i, RED[w][u]), u))


def send_mask(i, w, t):
    on = [u for u in order(i, w) if hops(i, RED[w][u]) == 0]
    off = [u for u in order(i, w) if hops(i, RED[w][u]) > 0]
    if t in on:
        n = 8 // len(on)
        return ((1 << n) - 1) << (8 + n * on.index(t))
    j = off.index(t)
    if len(off) == 8:
        return 1 << j
    return 3 if j == 0 else 1 << (j + 1)


def rank_program(g, core, T, topo):
    cores = list(T.cores)
    rank = T.rank_of(core)

    def dst_id(d):
        rid, pid = topo.addr(d, core)
        return DstId(rid=rid, pnc=pid)
    res = [T.sem.res0, T.sem.res1]
    ss, ps, rs = [T.s0, T.s1], [T.p0, T.p1], [T.r0, T.r1]
    if rank is not None:
        lds = [T.sem.ld0, T.sem.ld1]
        qs = [g.sync, g.scalar]
        rows = [(0, ROWS[0]), (ROWS[0], 32)]
        for w in range(NW):
            g.sync.dma_start(ss[w][:], T.x[rows[w][0]:rows[w][1]]).then_inc(lds[w], 16)
        for w in range(NW):
            g.wait_ge(lds[w], 16)
            trs = []
            for t in order(rank, w):
                trs.append(RemoteDMATransfer(dst_ids=[dst_id(RED[w][t])], dma_engine_mask=send_mask(rank, w, t), remote_sem=T.sem.arrived, src=ss[w][t], dst=ps[w][rank]))
            g.remote_dma_fused(trs, local_sem=T.sem.sent)
        for w in range(NW):
            qs[w].wait_ge(res[w], 8 * PWS[w])
            qs[w].dma_start(T.y[rows[w][0]:rows[w][1]], rs[w][:]).then_inc(T.sem.stored, 16)
        g.wait_ge(T.sem.sent, sum(bits(send_mask(rank, w, t)) for w in range(NW) for t in range(PWS[w])))
        g.wait_ge(T.sem.stored, 16 * NW)
        return
    mine = [(w, t) for w in range(NW) for t in range(PWS[w]) if RED[w][t] == core]
    if not mine:
        return
    w, t = mine[0]
    g.wait_ge(T.sem.arrived, sum(bits(send_mask(i, w, t)) for i in range(R)))
    srcs = [ps[w][i] for i in range(R)]
    away = [c for c in cores if c // 8 != core // 8]
    home = [c for c in cores if c // 8 == core // 8]
    trs = [RemoteDMATransfer(dst_ids=[dst_id(c) for c in away], dma_engine_mask=0xFF, remote_sem=res[w], srcs=srcs, dsts=[rs[w][t] for c in away], alu_op=1)]
    if home:
        trs.append(RemoteDMATransfer(dst_ids=[dst_id(c) for c in home], dma_engine_mask=0xFF00, remote_sem=res[w], srcs=srcs, dsts=[rs[w][t] for c in home], alu_op=1))
    g.remote_dma_fused(trs, local_sem=T.sem.sent)
    g.wait_ge(T.sem.sent, 8 * len(trs))
